import numpy as np
import ml_dtypes

BF16 = ml_dtypes.bfloat16


def bf(x):
    return np.asarray(x, np.float32).astype(BF16)


def f32(x):
    return np.asarray(x, np.float32)


def f64(x):
    return np.asarray(x).astype(np.float64)


def striped(idx):
    return np.concatenate([l.reshape(-1, 16).T for l in idx])


def rows(idx, k):
    return np.tile(np.repeat(idx, 16, axis=0), (k // (16 * 8), 1))


def look(tab, idx):
    return np.take_along_axis(f64(tab), rows(idx, len(tab)), axis=1)


K, S, V, N = 512, 2048, 2048, 2048


def angles():
    a = np.random.uniform(0.0, 2.0 * np.pi, (K, S))
    return np.stack([np.cos(a), np.sin(a)])


def setup_inputs():
    return {"tab": bf(angles()), "x0": bf(np.random.standard_normal((K, V))), "x1": bf(np.random.standard_normal((K, V))), "offs": striped(np.random.randint(0, S, (8, N)))}


def reference(tab, x0, x1, offs):
    idx = np.stack([g.T.reshape(-1) for g in np.split(offs, 8)])
    x = f64(x0) * look(tab[0], idx) + f64(x1) * look(tab[1], idx)
    return x

@@ -1,0 +1,57 @@
+import concourse.mybir as mybir
+from concourse.masks import make_identity
+
+BF16, F32, U16 = mybir.dt.bfloat16, mybir.dt.float32, mybir.dt.uint16
+MULT = mybir.AluOpType.mult
+
+P = 128
+PIECE = 512
+ENTRIES_PER_COLUMN = 16
+
+
+def tile_lookup_rope_mul_out_kernel(tc, tab, x0, x1, offs, out):
+    nc = tc.nc
+    rows, entries = out.shape
+    positions = tab.shape[2]
+    blocks = rows // P
+    pieces = entries // PIECE
+    piece_columns = PIECE // ENTRIES_PER_COLUMN
+
+    with (
+        tc.tile_pool(name="held", bufs=1) as held,
+        tc.tile_pool(name="tables", bufs=blocks) as tables,
+        tc.tile_pool(name="streams", bufs=blocks) as streams,
+        tc.tile_pool(name="products", bufs=2 * pieces) as products,
+        tc.tile_pool(name="results", bufs=4) as results,
+        tc.psum_pool(name="sums", bufs=4) as sums,
+    ):
+        offsets = held.tile([P, entries // ENTRIES_PER_COLUMN], U16)
+        nc.sync.dma_start(offsets[:], offs)
+        identity = held.tile([P, P], BF16)
+        make_identity(nc, identity[:])
+
+        for b in range(blocks):
+            block = slice(b * P, (b + 1) * P)
+            cosines = tables.tile([P, positions], BF16)
+            nc.sync.dma_start(cosines[:], tab[0, block, :])
+            x0_rows = streams.tile([P, entries], BF16)
+            nc.sync.dma_start(x0_rows[:], x0[block, :])
+            sines = tables.tile([P, positions], BF16)
+            nc.sync.dma_start(sines[:], tab[1, block, :])
+            x1_rows = streams.tile([P, entries], BF16)
+            nc.sync.dma_start(x1_rows[:], x1[block, :])
+
+            for k in range(pieces):
+                cols = slice(k * PIECE, (k + 1) * PIECE)
+                piece_list = offsets[:, k * piece_columns : (k + 1) * piece_columns]
+                x_cos = products.tile([P, PIECE], BF16)
+                nc.vector.tensor_tensor(x_cos[:], cosines[:].indirect(piece_list), x0_rows[:, cols], MULT)
+                x_sin = products.tile([P, PIECE], BF16)
+                nc.vector.tensor_tensor(x_sin[:], sines[:].indirect(piece_list), x1_rows[:, cols], MULT)
+
+                total = sums.tile([P, PIECE], F32)
+                nc.tensor.matmul(total[:], identity[:], x_cos[:], start=True, stop=False)
+                nc.tensor.matmul(total[:], identity[:], x_sin[:], start=False, stop=True)
+                result = results.tile([P, PIECE], F32)
+                nc.scalar.copy(result[:], total[:])
+                nc.scalar.dma_start(out[block, cols], result[:])

@@ -21,7 +21,7 @@ def tile_lookup_rope_mul_out_kernel(tc, tab, x0, x1, offs, out):
         tc.tile_pool(name="held", bufs=1) as held,
         tc.tile_pool(name="tables", bufs=blocks) as tables,
         tc.tile_pool(name="streams", bufs=blocks) as streams,
-        tc.tile_pool(name="products", bufs=2 * pieces) as products,
+        tc.tile_pool(name="products", bufs=4) as products,
         tc.tile_pool(name="results", bufs=4) as results,
         tc.psum_pool(name="sums", bufs=4) as sums,
     ):
@@ -32,25 +32,30 @@ def tile_lookup_rope_mul_out_kernel(tc, tab, x0, x1, offs, out):
 
         for b in range(blocks):
             block = slice(b * P, (b + 1) * P)
+            first = b == 0
             cosines = tables.tile([P, positions], BF16)
-            nc.sync.dma_start(cosines[:], tab[0, block, :])
+            (nc.scalar if first else nc.sync).dma_start(cosines[:], tab[0, block, :])
             x0_rows = streams.tile([P, entries], BF16)
-            nc.sync.dma_start(x0_rows[:], x0[block, :])
+            for cols in [slice(0, PIECE), slice(PIECE, entries)] if first else [slice(0, entries)]:
+                nc.sync.dma_start(x0_rows[:, cols], x0[block, cols])
             sines = tables.tile([P, positions], BF16)
             nc.sync.dma_start(sines[:], tab[1, block, :])
             x1_rows = streams.tile([P, entries], BF16)
             nc.sync.dma_start(x1_rows[:], x1[block, :])
 
+            x_cos = products.tile([P, entries], BF16)
             for k in range(pieces):
                 cols = slice(k * PIECE, (k + 1) * PIECE)
                 piece_list = offsets[:, k * piece_columns : (k + 1) * piece_columns]
-                x_cos = products.tile([P, PIECE], BF16)
-                nc.vector.tensor_tensor(x_cos[:], cosines[:].indirect(piece_list), x0_rows[:, cols], MULT)
+                nc.vector.tensor_tensor(x_cos[:, cols], cosines[:].indirect(piece_list), x0_rows[:, cols], MULT)
+            for k in range(pieces):
+                cols = slice(k * PIECE, (k + 1) * PIECE)
+                piece_list = offsets[:, k * piece_columns : (k + 1) * piece_columns]
                 x_sin = products.tile([P, PIECE], BF16)
                 nc.vector.tensor_tensor(x_sin[:], sines[:].indirect(piece_list), x1_rows[:, cols], MULT)
 
                 total = sums.tile([P, PIECE], F32)
-                nc.tensor.matmul(total[:], identity[:], x_cos[:], start=True, stop=False)
+                nc.tensor.matmul(total[:], identity[:], x_cos[:, cols], start=True, stop=False)
                 nc.tensor.matmul(total[:], identity[:], x_sin[:], start=False, stop=True)
                 result = results.tile([P, PIECE], F32)
                 nc.scalar.copy(result[:], total[:])

import concourse.mybir as mybir
from concourse.masks import make_identity

BF16, F32, U16 = mybir.dt.bfloat16, mybir.dt.float32, mybir.dt.uint16
MULT = mybir.AluOpType.mult

P = 128
PIECE = 512
ENTRIES_PER_COLUMN = 16


def tile_lookup_rope_mul_out_kernel(tc, tab, x0, x1, offs, out):
    nc = tc.nc
    rows, entries = out.shape
    positions = tab.shape[2]
    blocks = rows // P
    pieces = entries // PIECE
    piece_columns = PIECE // ENTRIES_PER_COLUMN

    with (
        tc.tile_pool(name="held", bufs=1) as held,
        tc.tile_pool(name="tables", bufs=blocks) as tables,
        tc.tile_pool(name="streams", bufs=blocks) as streams,
        tc.tile_pool(name="products", bufs=4) as products,
        tc.tile_pool(name="results", bufs=4) as results,
        tc.psum_pool(name="sums", bufs=4) as sums,
    ):
        offsets = held.tile([P, entries // ENTRIES_PER_COLUMN], U16)
        nc.sync.dma_start(offsets[:], offs)
        identity = held.tile([P, P], BF16)
        make_identity(nc, identity[:])

        for b in range(blocks):
            block = slice(b * P, (b + 1) * P)
            first = b == 0
            cosines = tables.tile([P, positions], BF16)
            (nc.scalar if first else nc.sync).dma_start(cosines[:], tab[0, block, :])
            x0_rows = streams.tile([P, entries], BF16)
            for cols in [slice(0, PIECE), slice(PIECE, entries)] if first else [slice(0, entries)]:
                nc.sync.dma_start(x0_rows[:, cols], x0[block, cols])
            sines = tables.tile([P, positions], BF16)
            nc.sync.dma_start(sines[:], tab[1, block, :])
            x1_rows = streams.tile([P, entries], BF16)
            nc.sync.dma_start(x1_rows[:], x1[block, :])

            x_cos = products.tile([P, entries], BF16)
            for k in range(pieces):
                cols = slice(k * PIECE, (k + 1) * PIECE)
                piece_list = offsets[:, k * piece_columns : (k + 1) * piece_columns]
                nc.vector.tensor_tensor(x_cos[:, cols], cosines[:].indirect(piece_list), x0_rows[:, cols], MULT)
            for k in range(pieces):
                cols = slice(k * PIECE, (k + 1) * PIECE)
                piece_list = offsets[:, k * piece_columns : (k + 1) * piece_columns]
                x_sin = products.tile([P, PIECE], BF16)
                nc.vector.tensor_tensor(x_sin[:], sines[:].indirect(piece_list), x1_rows[:, cols], MULT)

                total = sums.tile([P, PIECE], F32)
                nc.tensor.matmul(total[:], identity[:], x_cos[:, cols], start=True, stop=False)
                nc.tensor.matmul(total[:], identity[:], x_sin[:], start=False, stop=True)
                result = results.tile([P, PIECE], F32)
                nc.scalar.copy(result[:], total[:])
                nc.scalar.dma_start(out[block, cols], result[:])
